import numpy as np
import ml_dtypes


def mxq(x, axis, fmt="e4m3"):
    dtype, down = {"e4m3": (ml_dtypes.float8_e4m3fn, 7), "e5m2": (ml_dtypes.float8_e5m2, 14)}[fmt]
    v = np.moveaxis(np.asarray(x, np.float32).astype(ml_dtypes.bfloat16).astype(np.float64), axis, -1)
    blocks = v.reshape(v.shape[:-1] + (-1, 32))
    amax = np.abs(blocks).max(-1, keepdims=True)
    byte = np.maximum(np.where(amax > 0, np.frexp(amax)[1] - 1 + 127, 0) - down, 1)
    scale = np.exp2(byte - 127.0)
    codes = (blocks / scale).astype(np.float32).astype(dtype).astype(np.float64)
    return np.moveaxis((codes * scale).reshape(v.shape), -1, axis)


WIDE = False


def mx_kscale(k):
    if not WIDE:
        return np.ones(k)
    levels = np.array([10, -10, 5, -5, 0])
    if k % 512:
        return np.exp2(np.random.permutation(np.resize(levels, k // 32))).repeat(32)
    a = np.empty((k // 512, 16))
    for p in range(k // 512):
        a[p, :8] = np.random.permutation(np.resize(levels, 8))
        for g in range(8):
            far = levels[np.abs(levels - a[p, g]) >= 10]
            a[p, g + 8] = far[np.random.randint(len(far))]
    return np.exp2(a.ravel()).repeat(32)


def f64(x):
    return np.asarray(x).astype(np.float64)


def striped(idx):
    return np.tile(idx.reshape(-1, 16).T, (8, 1)).astype(np.uint16)


def unstriped(offs):
    return offs[:16].T.reshape(-1).astype(np.int64)


def pack_weight(w):
    k, n = w.shape
    w = f64(np.asarray(w, np.float32).astype(ml_dtypes.bfloat16)).reshape(k // 32, 32, n)
    amax = np.abs(w).max(1)
    byte = np.clip(np.where(amax > 0, np.frexp(amax)[1] - 1 + 127 - 7, 1), 1, 254)
    scaled = (w * np.exp2(127.0 - byte)[:, None, :]).reshape(k, n).astype(np.float32)
    words = np.ascontiguousarray(scaled.reshape(k // 512, 128, 4, n).transpose(0, 1, 3, 2)).astype(ml_dtypes.float8_e4m3fn).view(np.uint8)
    return words, np.ascontiguousarray(byte.astype(np.uint8).reshape(k // 512, 16, n))


def unpack_weight(words, scales):
    g, p, n, _ = words.shape
    vals = np.ascontiguousarray(words).view(ml_dtypes.float8_e4m3fn).astype(np.float64) * np.repeat(np.exp2(scales.astype(np.float64) - 127.0), 8, axis=1)[..., None]
    return vals.transpose(0, 1, 3, 2).reshape(g * 512, n)


K, T, E, C, N = 1536, 512, 8, 128, 128


def by_expert(wq, xq):
    return np.concatenate([wq[e].T @ xq[:, e * C:(e + 1) * C] for e in range(E)], axis=1)


def setup_inputs():
    n = np.random.standard_normal
    s = mx_kscale(K)[:, None]
    first = np.random.permutation(np.repeat(np.arange(E), T // E))
    second = (first + 1 + np.random.permutation(np.repeat(np.arange(E - 1), -(-T // (E - 1)))[:T])) % E
    while np.bincount(second, minlength=E).max() != T // E:
        load = np.bincount(second, minlength=E); hi, lo = int(load.argmax()), int(load.argmin())
        t = np.flatnonzero((second == hi) & (first != lo))[0]; second[t] = lo
    slot_token = np.empty(E * C, np.int64); pos = np.empty((2, T), np.int64); fill = np.zeros(E, np.int64)
    place = np.stack([np.random.permutation(C) for _ in range(E)])
    for r, deal in enumerate((first, second)):
        for t in np.random.permutation(T):
            e = deal[t]; j = e * C + place[e, fill[e]]; fill[e] += 1; slot_token[j] = t; pos[r, t] = j
    g = np.random.uniform(0.2, 0.8, T)
    packed = [pack_weight(m) for m in n((E, K, N)) / np.sqrt(K) / s[None]]
    return {
        "xT": (n((K, T)) * s).astype(np.float32),
        "w_words": np.stack([m[0] for m in packed]),
        "w_scales": np.stack([m[1] for m in packed]),
        "b": (0.3 * n((N, E))).astype(np.float32),
        "gate": np.stack([np.tile(g, (N, 1)), np.tile(1.0 - g, (N, 1))]).astype(np.float32),
        "offs": striped(slot_token),
        "pos1": striped(pos[0]),
        "pos2": striped(pos[1]),
    }


def reference(xT, w_words, w_scales, b, gate, offs, pos1, pos2):
    idx = unstriped(offs)
    xq = mxq(f64(xT)[:, idx], 0, "e4m3")
    w = np.stack([unpack_weight(w_words[e], w_scales[e]) for e in range(E)])
    y = by_expert(w, xq)
    y = y + np.repeat(f64(b), C, axis=1)
    return f64(gate[0]) * y[:, unstriped(pos1)] + f64(gate[1]) * y[:, unstriped(pos2)]

@@ -1,0 +1,145 @@
+from contextlib import ExitStack
+
+import concourse.mybir as mybir
+
+F32 = mybir.dt.float32
+BF16 = mybir.dt.bfloat16
+I32 = mybir.dt.int32
+U32 = mybir.dt.uint32
+U16 = mybir.dt.uint16
+U8 = mybir.dt.uint8
+FP8X4 = mybir.dt.float8_e4m3fn_x4
+MULT = mybir.AluOpType.mult
+ADD = mybir.AluOpType.add
+IDENTITY = mybir.ActivationFunctionType.Identity
+
+P = 128
+K, T, E, C, N = 1536, 512, 8, 128, 128
+SLOTS = E * C
+PASSES = K // 512
+FLOPS = 2 * K * N * SLOTS
+WINDOW = 1408
+CHUNKS = (((0, 256), (256, 512)), ((0, 512),), ((0, 512),))
+VECTOR_TOKENS = (168, 192, 0)
+LAST_CUTS = (0, 384, 768, 1024)
+
+
+def interleave(copy, grouped, raw, lo, hi):
+    copy(
+        out=grouped[:, lo:hi, :].rearrange("p (c i) j -> p c j i", i=4),
+        in_=raw[:, :, lo:hi].rearrange("p j (c i) -> p c j i", i=4),
+    )
+
+
+def tile_routed_moe_kernel(tc, xT, w_words, w_scales, b, gate, offs, pos1, pos2, out):
+    nc = tc.nc
+    with ExitStack() as ctx:
+        keep = ctx.enter_context(tc.tile_pool(name="keep", bufs=1))
+        psum = ctx.enter_context(tc.psum_pool(name="psum", bufs=1))
+
+        offs_sb = keep.tile([P, SLOTS // 16], U16, name="offs_sb")
+        pos1_sb = keep.tile([P, T // 16], U16, name="pos1_sb")
+        pos2_sb = keep.tile([P, T // 16], U16, name="pos2_sb")
+
+        raw = [keep.tile([P, 4, T], F32, name=f"raw{a}") for a in range(PASSES)]
+        grouped = [keep.tile([P, T, 4], BF16, name=f"grouped{a}", align_bytes=64) for a in range(PASSES)]
+        words = [keep.tile([P, WINDOW], I32, name=f"words{a}", align_bytes=64) for a in range(PASSES)]
+        scales = keep.tile([P, WINDOW], U8, name="scales", align_bytes=64)
+        slot_words = [keep.tile([P, SLOTS], U32, name=f"slot_words{a}", align_bytes=64) for a in range(PASSES)]
+        slot_scales = keep.tile([P, SLOTS], U8, name="slot_scales", align_bytes=64)
+        wq = [keep.tile([P, E * N], U32, name=f"wq{a}", align_bytes=64) for a in range(PASSES)]
+        wq_scales = keep.tile([P, E * PASSES * N], U8, name="wq_scales", align_bytes=64)
+        bias = keep.tile([P, E], F32, name="bias")
+        gates = keep.tile([P, 2, T], F32, name="gates")
+        y = keep.tile([P, SLOTS], F32, name="y")
+        part1 = keep.tile([P, T], F32, name="part1")
+        part2 = keep.tile([P, T], F32, name="part2")
+        total = keep.tile([P, T], F32, name="total")
+        warm = keep.tile([P, 1], F32, name="warm")
+
+        def load_x(a):
+            rows = xT[512 * a : 512 * (a + 1), :].rearrange("(p j) w -> p j w", j=4)
+            for lo, hi in CHUNKS[a]:
+                nc.sync.dma_start(out=raw[a][:, :, lo:hi], in_=rows[:, :, lo:hi])
+
+        load_x(0)
+        nc.sync.dma_start(offs_sb[:], offs)
+        load_x(1)
+        load_x(2)
+
+        nc.vector.memset(wq_scales[:].bitcast(I32), 0)
+        nc.vector.memset(warm[:], 0.0)
+        nc.scalar.activation(out=warm[:], in_=warm[:], func=IDENTITY)
+        nc.gpsimd.memset(scales[:], 0)
+        for a in range(PASSES):
+            nc.vector.memset(words[a][:, T:], 0)
+
+        for q in range(4):
+            nc.sync.dma_start(
+                out=wq_scales[32 * q : 32 * q + 4, :].bitcast(I32).rearrange("r (g n) -> r g n", g=E * PASSES),
+                in_=w_scales[:, :, 4 * q : 4 * q + 4, :].bitcast(I32).rearrange("e a r n -> r (e a) n"),
+            )
+        for a in range(PASSES):
+            nc.sync.dma_start(
+                out=wq[a][:].bitcast(I32).rearrange("p (e n) -> p e n", e=E),
+                in_=w_words[:, a].rearrange("e p n r -> p e (n r)").bitcast(I32),
+            )
+            if a == 0:
+                nc.sync.dma_start(out=bias[:], in_=b)
+                nc.sync.dma_start(pos1_sb[:], pos1)
+                nc.sync.dma_start(pos2_sb[:], pos2)
+        nc.sync.dma_start(out=gates[:], in_=gate.rearrange("g p t -> p g t"))
+
+        acc = [psum.tile([P, C], F32, name=f"acc{e}") for e in range(E)]
+
+        def multiply(a, e):
+            slots = slice(e * C, (e + 1) * C)
+            weight = slice((e * PASSES + a) * N, (e * PASSES + a + 1) * N)
+            nc.tensor.matmul_mx(
+                out=acc[e][:],
+                lhsT=wq[a][:, e * N : (e + 1) * N].bitcast(FP8X4),
+                lhsT_scale=wq_scales[:, weight],
+                rhs=slot_words[a][:, slots].bitcast(FP8X4),
+                rhs_scale=slot_scales[4 * a : P, slots],
+                start=(a == 0),
+                stop=(a == PASSES - 1),
+            )
+
+        def gather_words(a, lo, hi):
+            nc.vector.tensor_copy(
+                out=slot_words[a][:, lo:hi],
+                in_=words[a][:].bitcast(U32).indirect(offs_sb[:, lo // 16 : hi // 16]),
+            )
+
+        for a in range(PASSES):
+            for lo, hi in CHUNKS[a]:
+                cut = lo + VECTOR_TOKENS[a]
+                if lo < cut:
+                    interleave(nc.vector.tensor_copy, grouped[a], raw[a], lo, cut)
+                interleave(nc.scalar.copy, grouped[a], raw[a], cut, hi)
+                nc.vector.quantize_mx(
+                    out=words[a][:, lo:hi].bitcast(FP8X4),
+                    scales=scales[4 * a : P, lo:hi],
+                    in_=grouped[a][:, lo:hi, :].rearrange("p t j -> p (t j)"),
+                )
+            if a < PASSES - 1:
+                gather_words(a, 0, SLOTS)
+
+        nc.vector.tensor_copy(out=slot_scales[:], in_=scales[:].indirect(offs_sb[:]))
+        for a in range(PASSES - 1):
+            for e in range(E):
+                multiply(a, e)
+        for lo, hi in zip(LAST_CUTS[:-1], LAST_CUTS[1:]):
+            gather_words(PASSES - 1, lo, hi)
+            for e in range(lo // C, hi // C):
+                multiply(PASSES - 1, e)
+                cols = slice(e * C, (e + 1) * C)
+                if e < E - 1:
+                    nc.scalar.activation(out=y[:, cols], in_=acc[e][:], func=IDENTITY, bias=bias[:, e : e + 1])
+                else:
+                    nc.vector.tensor_scalar(out=y[:, cols], in0=acc[e][:], scalar1=bias[:, e : e + 1], scalar2=None, op0=ADD)
+
+        nc.vector.tensor_tensor(out=part1[:], in0=y[:].indirect(pos1_sb[:]), in1=gates[:, 0, :], op=MULT)
+        nc.vector.tensor_tensor(out=part2[:], in0=y[:].indirect(pos2_sb[:]), in1=gates[:, 1, :], op=MULT)
+        nc.vector.tensor_tensor(out=total[:], in0=part1[:], in1=part2[:], op=ADD)
+        nc.sync.dma_start(out=out, in_=total[:])

@@ -18,9 +18,11 @@ K, T, E, C, N = 1536, 512, 8, 128, 128
 SLOTS = E * C
 PASSES = K // 512
 FLOPS = 2 * K * N * SLOTS
-WINDOW = 1408
-CHUNKS = (((0, 256), (256, 512)), ((0, 512),), ((0, 512),))
-VECTOR_TOKENS = (168, 192, 0)
+WINDOW = 1376
+HALVES = ((0, 256), (256, 512))
+CHUNKS = (HALVES, HALVES, HALVES)
+VECTOR_TOKENS = (144, 0, 0)
+SCALE_CUTS = (0, 512, 1024)
 LAST_CUTS = (0, 384, 768, 1024)
 
 
@@ -67,10 +69,10 @@ def tile_routed_moe_kernel(tc, xT, w_words, w_scales, b, gate, offs, pos1, pos2,
         load_x(1)
         load_x(2)
 
-        nc.vector.memset(wq_scales[:].bitcast(I32), 0)
-        nc.vector.memset(warm[:], 0.0)
+        nc.gpsimd.memset(warm[:], 0.0)
         nc.scalar.activation(out=warm[:], in_=warm[:], func=IDENTITY)
         nc.gpsimd.memset(scales[:], 0)
+        nc.gpsimd.memset(wq_scales[:].bitcast(I32), 0)
         for a in range(PASSES):
             nc.vector.memset(words[a][:, T:], 0)
 
@@ -116,7 +118,8 @@ def tile_routed_moe_kernel(tc, xT, w_words, w_scales, b, gate, offs, pos1, pos2,
                 cut = lo + VECTOR_TOKENS[a]
                 if lo < cut:
                     interleave(nc.vector.tensor_copy, grouped[a], raw[a], lo, cut)
-                interleave(nc.scalar.copy, grouped[a], raw[a], cut, hi)
+                if cut < hi:
+                    interleave(nc.scalar.copy, grouped[a], raw[a], cut, hi)
                 nc.vector.quantize_mx(
                     out=words[a][:, lo:hi].bitcast(FP8X4),
                     scales=scales[4 * a : P, lo:hi],
@@ -125,10 +128,11 @@ def tile_routed_moe_kernel(tc, xT, w_words, w_scales, b, gate, offs, pos1, pos2,
             if a < PASSES - 1:
                 gather_words(a, 0, SLOTS)
 
-        nc.vector.tensor_copy(out=slot_scales[:], in_=scales[:].indirect(offs_sb[:]))
-        for a in range(PASSES - 1):
-            for e in range(E):
-                multiply(a, e)
+        for lo, hi in zip(SCALE_CUTS[:-1], SCALE_CUTS[1:]):
+            nc.vector.tensor_copy(out=slot_scales[:, lo:hi], in_=scales[:].indirect(offs_sb[:, lo // 16 : hi // 16]))
+            for e in range(lo // C, hi // C):
+                for a in range(PASSES - 1):
+                    multiply(a, e)
         for lo, hi in zip(LAST_CUTS[:-1], LAST_CUTS[1:]):
             gather_words(PASSES - 1, lo, hi)
             for e in range(lo // C, hi // C):

@@ -18,10 +18,11 @@ K, T, E, C, N = 1536, 512, 8, 128, 128
 SLOTS = E * C
 PASSES = K // 512
 FLOPS = 2 * K * N * SLOTS
-WINDOW = 1376
-HALVES = ((0, 256), (256, 512))
-CHUNKS = (HALVES, HALVES, HALVES)
-VECTOR_TOKENS = (144, 0, 0)
+WORD_COLUMNS = (1376, 1376, 512)
+SCALE_COLUMNS = 704
+WHOLE = ((0, 512),)
+CHUNKS = (WHOLE, WHOLE, WHOLE)
+VECTOR_TOKENS = (320, 112, 0)
 SCALE_CUTS = (0, 512, 1024)
 LAST_CUTS = (0, 384, 768, 1024)
 
@@ -45,8 +46,8 @@ def tile_routed_moe_kernel(tc, xT, w_words, w_scales, b, gate, offs, pos1, pos2,
 
         raw = [keep.tile([P, 4, T], F32, name=f"raw{a}") for a in range(PASSES)]
         grouped = [keep.tile([P, T, 4], BF16, name=f"grouped{a}", align_bytes=64) for a in range(PASSES)]
-        words = [keep.tile([P, WINDOW], I32, name=f"words{a}", align_bytes=64) for a in range(PASSES)]
-        scales = keep.tile([P, WINDOW], U8, name="scales", align_bytes=64)
+        words = [keep.tile([P, WORD_COLUMNS[a]], I32, name=f"words{a}", align_bytes=64) for a in range(PASSES)]
+        scales = keep.tile([P, SCALE_COLUMNS], U8, name="scales", align_bytes=64)
         slot_words = [keep.tile([P, SLOTS], U32, name=f"slot_words{a}", align_bytes=64) for a in range(PASSES)]
         slot_scales = keep.tile([P, SLOTS], U8, name="slot_scales", align_bytes=64)
         wq = [keep.tile([P, E * N], U32, name=f"wq{a}", align_bytes=64) for a in range(PASSES)]
@@ -69,27 +70,30 @@ def tile_routed_moe_kernel(tc, xT, w_words, w_scales, b, gate, offs, pos1, pos2,
         load_x(1)
         load_x(2)
 
+        nc.scalar.dma_start(out=bias[:], in_=b)
         nc.gpsimd.memset(warm[:], 0.0)
         nc.scalar.activation(out=warm[:], in_=warm[:], func=IDENTITY)
-        nc.gpsimd.memset(scales[:], 0)
-        nc.gpsimd.memset(wq_scales[:].bitcast(I32), 0)
-        for a in range(PASSES):
-            nc.vector.memset(words[a][:, T:], 0)
+        nc.vector.memset(scales[:].bitcast(I32), 0)
+        nc.vector.memset(words[0][:, T:], 0)
+        nc.vector.memset(words[1][:, T:], 0)
+        nc.vector.memset(wq_scales[:].bitcast(I32), 0)
 
+        def load_w(a):
+            nc.sync.dma_start(
+                out=wq[a][:].bitcast(I32).rearrange("p (e n) -> p e n", e=E),
+                in_=w_words[:, a].rearrange("e p n r -> p e (n r)").bitcast(I32),
+            )
+
+        load_w(0)
         for q in range(4):
             nc.sync.dma_start(
                 out=wq_scales[32 * q : 32 * q + 4, :].bitcast(I32).rearrange("r (g n) -> r g n", g=E * PASSES),
                 in_=w_scales[:, :, 4 * q : 4 * q + 4, :].bitcast(I32).rearrange("e a r n -> r (e a) n"),
             )
-        for a in range(PASSES):
-            nc.sync.dma_start(
-                out=wq[a][:].bitcast(I32).rearrange("p (e n) -> p e n", e=E),
-                in_=w_words[:, a].rearrange("e p n r -> p e (n r)").bitcast(I32),
-            )
-            if a == 0:
-                nc.sync.dma_start(out=bias[:], in_=b)
-                nc.sync.dma_start(pos1_sb[:], pos1)
-                nc.sync.dma_start(pos2_sb[:], pos2)
+        load_w(1)
+        load_w(2)
+        nc.sync.dma_start(pos1_sb[:], pos1)
+        nc.sync.dma_start(pos2_sb[:], pos2)
         nc.sync.dma_start(out=gates[:], in_=gate.rearrange("g p t -> p g t"))
 
         acc = [psum.tile([P, C], F32, name=f"acc{e}") for e in range(E)]
@@ -144,6 +148,14 @@ def tile_routed_moe_kernel(tc, xT, w_words, w_scales, b, gate, offs, pos1, pos2,
                     nc.vector.tensor_scalar(out=y[:, cols], in0=acc[e][:], scalar1=bias[:, e : e + 1], scalar2=None, op0=ADD)
 
         nc.vector.tensor_tensor(out=part1[:], in0=y[:].indirect(pos1_sb[:]), in1=gates[:, 0, :], op=MULT)
-        nc.vector.tensor_tensor(out=part2[:], in0=y[:].indirect(pos2_sb[:]), in1=gates[:, 1, :], op=MULT)
-        nc.vector.tensor_tensor(out=total[:], in0=part1[:], in1=part2[:], op=ADD)
-        nc.sync.dma_start(out=out, in_=total[:])
+        halves = ((0, 256), (256, 512))
+        for lo, hi in halves:
+            nc.vector.tensor_tensor(
+                out=part2[:, lo:hi],
+                in0=y[:].indirect(pos2_sb[:, lo // 16 : hi // 16]),
+                in1=gates[:, 1, lo:hi],
+                op=MULT,
+            )
+        for lo, hi in halves:
+            nc.vector.tensor_tensor(out=total[:, lo:hi], in0=part1[:, lo:hi], in1=part2[:, lo:hi], op=ADD)
+            nc.sync.dma_start(out=out[:, lo:hi], in_=total[:, lo:hi])

@@ -20,9 +20,8 @@ PASSES = K // 512
 FLOPS = 2 * K * N * SLOTS
 WORD_COLUMNS = (1376, 1376, 512)
 SCALE_COLUMNS = 704
-WHOLE = ((0, 512),)
-CHUNKS = (WHOLE, WHOLE, WHOLE)
-VECTOR_TOKENS = (320, 112, 0)
+HALVES = ((0, 256), (256, 512))
+VECTOR_TOKENS = ((128, 128), (0, 64), (0, 0))
 SCALE_CUTS = (0, 512, 1024)
 LAST_CUTS = (0, 384, 768, 1024)
 
@@ -62,7 +61,7 @@ def tile_routed_moe_kernel(tc, xT, w_words, w_scales, b, gate, offs, pos1, pos2,
 
         def load_x(a):
             rows = xT[512 * a : 512 * (a + 1), :].rearrange("(p j) w -> p j w", j=4)
-            for lo, hi in CHUNKS[a]:
+            for lo, hi in HALVES:
                 nc.sync.dma_start(out=raw[a][:, :, lo:hi], in_=rows[:, :, lo:hi])
 
         load_x(0)
@@ -118,8 +117,8 @@ def tile_routed_moe_kernel(tc, xT, w_words, w_scales, b, gate, offs, pos1, pos2,
             )
 
         for a in range(PASSES):
-            for lo, hi in CHUNKS[a]:
-                cut = lo + VECTOR_TOKENS[a]
+            for (lo, hi), share in zip(HALVES, VECTOR_TOKENS[a]):
+                cut = lo + share
                 if lo < cut:
                     interleave(nc.vector.tensor_copy, grouped[a], raw[a], lo, cut)
                 if cut < hi:
@@ -142,20 +141,19 @@ def tile_routed_moe_kernel(tc, xT, w_words, w_scales, b, gate, offs, pos1, pos2,
             for e in range(lo // C, hi // C):
                 multiply(PASSES - 1, e)
                 cols = slice(e * C, (e + 1) * C)
-                if e < E - 1:
+                if e < E - 2:
                     nc.scalar.activation(out=y[:, cols], in_=acc[e][:], func=IDENTITY, bias=bias[:, e : e + 1])
                 else:
                     nc.vector.tensor_scalar(out=y[:, cols], in0=acc[e][:], scalar1=bias[:, e : e + 1], scalar2=None, op0=ADD)
 
         nc.vector.tensor_tensor(out=part1[:], in0=y[:].indirect(pos1_sb[:]), in1=gates[:, 0, :], op=MULT)
-        halves = ((0, 256), (256, 512))
-        for lo, hi in halves:
+        for lo, hi in HALVES:
             nc.vector.tensor_tensor(
                 out=part2[:, lo:hi],
                 in0=y[:].indirect(pos2_sb[:, lo // 16 : hi // 16]),
                 in1=gates[:, 1, lo:hi],
                 op=MULT,
             )
-        for lo, hi in halves:
+        for lo, hi in HALVES:
             nc.vector.tensor_tensor(out=total[:, lo:hi], in0=part1[:, lo:hi], in1=part2[:, lo:hi], op=ADD)
             nc.sync.dma_start(out=out[:, lo:hi], in_=total[:, lo:hi])

@@ -21,7 +21,8 @@ FLOPS = 2 * K * N * SLOTS
 WORD_COLUMNS = (1376, 1376, 512)
 SCALE_COLUMNS = 704
 HALVES = ((0, 256), (256, 512))
-VECTOR_TOKENS = ((128, 128), (0, 64), (0, 0))
+VECTOR_TOKENS = ((128, 128), (0, 0), (0, 0))
+LOADS = (((0, 512),), HALVES, HALVES)
 SCALE_CUTS = (0, 512, 1024)
 LAST_CUTS = (0, 384, 768, 1024)
 
@@ -61,7 +62,7 @@ def tile_routed_moe_kernel(tc, xT, w_words, w_scales, b, gate, offs, pos1, pos2,
 
         def load_x(a):
             rows = xT[512 * a : 512 * (a + 1), :].rearrange("(p j) w -> p j w", j=4)
-            for lo, hi in HALVES:
+            for lo, hi in LOADS[a]:
                 nc.sync.dma_start(out=raw[a][:, :, lo:hi], in_=rows[:, :, lo:hi])
 
         load_x(0)
@@ -110,6 +111,13 @@ def tile_routed_moe_kernel(tc, xT, w_words, w_scales, b, gate, offs, pos1, pos2,
                 stop=(a == PASSES - 1),
             )
 
+        def quantize(a, lo, hi):
+            nc.vector.quantize_mx(
+                out=words[a][:, lo:hi].bitcast(FP8X4),
+                scales=scales[4 * a : P, lo:hi],
+                in_=grouped[a][:, lo:hi, :].rearrange("p t j -> p (t j)"),
+            )
+
         def gather_words(a, lo, hi):
             nc.vector.tensor_copy(
                 out=slot_words[a][:, lo:hi],
@@ -123,13 +131,12 @@ def tile_routed_moe_kernel(tc, xT, w_words, w_scales, b, gate, offs, pos1, pos2,
                     interleave(nc.vector.tensor_copy, grouped[a], raw[a], lo, cut)
                 if cut < hi:
                     interleave(nc.scalar.copy, grouped[a], raw[a], cut, hi)
-                nc.vector.quantize_mx(
-                    out=words[a][:, lo:hi].bitcast(FP8X4),
-                    scales=scales[4 * a : P, lo:hi],
-                    in_=grouped[a][:, lo:hi, :].rearrange("p t j -> p (t j)"),
-                )
+                if a < PASSES - 1:
+                    quantize(a, lo, hi)
             if a < PASSES - 1:
                 gather_words(a, 0, SLOTS)
+            else:
+                quantize(a, 0, T)
 
         for lo, hi in zip(SCALE_CUTS[:-1], SCALE_CUTS[1:]):
             nc.vector.tensor_copy(out=slot_scales[:, lo:hi], in_=scales[:].indirect(offs_sb[:, lo // 16 : hi // 16]))

from contextlib import ExitStack

import concourse.mybir as mybir

F32 = mybir.dt.float32
BF16 = mybir.dt.bfloat16
I32 = mybir.dt.int32
U32 = mybir.dt.uint32
U16 = mybir.dt.uint16
U8 = mybir.dt.uint8
FP8X4 = mybir.dt.float8_e4m3fn_x4
MULT = mybir.AluOpType.mult
ADD = mybir.AluOpType.add
IDENTITY = mybir.ActivationFunctionType.Identity

P = 128
K, T, E, C, N = 1536, 512, 8, 128, 128
SLOTS = E * C
PASSES = K // 512
FLOPS = 2 * K * N * SLOTS
WORD_COLUMNS = (1376, 1376, 512)
SCALE_COLUMNS = 704
HALVES = ((0, 256), (256, 512))
VECTOR_TOKENS = ((128, 128), (0, 0), (0, 0))
LOADS = (((0, 512),), HALVES, HALVES)
SCALE_CUTS = (0, 512, 1024)
LAST_CUTS = (0, 384, 768, 1024)


def interleave(copy, grouped, raw, lo, hi):
    copy(
        out=grouped[:, lo:hi, :].rearrange("p (c i) j -> p c j i", i=4),
        in_=raw[:, :, lo:hi].rearrange("p j (c i) -> p c j i", i=4),
    )


def tile_routed_moe_kernel(tc, xT, w_words, w_scales, b, gate, offs, pos1, pos2, out):
    nc = tc.nc
    with ExitStack() as ctx:
        keep = ctx.enter_context(tc.tile_pool(name="keep", bufs=1))
        psum = ctx.enter_context(tc.psum_pool(name="psum", bufs=1))

        offs_sb = keep.tile([P, SLOTS // 16], U16, name="offs_sb")
        pos1_sb = keep.tile([P, T // 16], U16, name="pos1_sb")
        pos2_sb = keep.tile([P, T // 16], U16, name="pos2_sb")

        raw = [keep.tile([P, 4, T], F32, name=f"raw{a}") for a in range(PASSES)]
        grouped = [keep.tile([P, T, 4], BF16, name=f"grouped{a}", align_bytes=64) for a in range(PASSES)]
        words = [keep.tile([P, WORD_COLUMNS[a]], I32, name=f"words{a}", align_bytes=64) for a in range(PASSES)]
        scales = keep.tile([P, SCALE_COLUMNS], U8, name="scales", align_bytes=64)
        slot_words = [keep.tile([P, SLOTS], U32, name=f"slot_words{a}", align_bytes=64) for a in range(PASSES)]
        slot_scales = keep.tile([P, SLOTS], U8, name="slot_scales", align_bytes=64)
        wq = [keep.tile([P, E * N], U32, name=f"wq{a}", align_bytes=64) for a in range(PASSES)]
        wq_scales = keep.tile([P, E * PASSES * N], U8, name="wq_scales", align_bytes=64)
        bias = keep.tile([P, E], F32, name="bias")
        gates = keep.tile([P, 2, T], F32, name="gates")
        y = keep.tile([P, SLOTS], F32, name="y")
        part1 = keep.tile([P, T], F32, name="part1")
        part2 = keep.tile([P, T], F32, name="part2")
        total = keep.tile([P, T], F32, name="total")
        warm = keep.tile([P, 1], F32, name="warm")

        def load_x(a):
            rows = xT[512 * a : 512 * (a + 1), :].rearrange("(p j) w -> p j w", j=4)
            for lo, hi in LOADS[a]:
                nc.sync.dma_start(out=raw[a][:, :, lo:hi], in_=rows[:, :, lo:hi])

        load_x(0)
        nc.sync.dma_start(offs_sb[:], offs)
        load_x(1)
        load_x(2)

        nc.scalar.dma_start(out=bias[:], in_=b)
        nc.gpsimd.memset(warm[:], 0.0)
        nc.scalar.activation(out=warm[:], in_=warm[:], func=IDENTITY)
        nc.vector.memset(scales[:].bitcast(I32), 0)
        nc.vector.memset(words[0][:, T:], 0)
        nc.vector.memset(words[1][:, T:], 0)
        nc.vector.memset(wq_scales[:].bitcast(I32), 0)

        def load_w(a):
            nc.sync.dma_start(
                out=wq[a][:].bitcast(I32).rearrange("p (e n) -> p e n", e=E),
                in_=w_words[:, a].rearrange("e p n r -> p e (n r)").bitcast(I32),
            )

        load_w(0)
        for q in range(4):
            nc.sync.dma_start(
                out=wq_scales[32 * q : 32 * q + 4, :].bitcast(I32).rearrange("r (g n) -> r g n", g=E * PASSES),
                in_=w_scales[:, :, 4 * q : 4 * q + 4, :].bitcast(I32).rearrange("e a r n -> r (e a) n"),
            )
        load_w(1)
        load_w(2)
        nc.sync.dma_start(pos1_sb[:], pos1)
        nc.sync.dma_start(pos2_sb[:], pos2)
        nc.sync.dma_start(out=gates[:], in_=gate.rearrange("g p t -> p g t"))

        acc = [psum.tile([P, C], F32, name=f"acc{e}") for e in range(E)]

        def multiply(a, e):
            slots = slice(e * C, (e + 1) * C)
            weight = slice((e * PASSES + a) * N, (e * PASSES + a + 1) * N)
            nc.tensor.matmul_mx(
                out=acc[e][:],
                lhsT=wq[a][:, e * N : (e + 1) * N].bitcast(FP8X4),
                lhsT_scale=wq_scales[:, weight],
                rhs=slot_words[a][:, slots].bitcast(FP8X4),
                rhs_scale=slot_scales[4 * a : P, slots],
                start=(a == 0),
                stop=(a == PASSES - 1),
            )

        def quantize(a, lo, hi):
            nc.vector.quantize_mx(
                out=words[a][:, lo:hi].bitcast(FP8X4),
                scales=scales[4 * a : P, lo:hi],
                in_=grouped[a][:, lo:hi, :].rearrange("p t j -> p (t j)"),
            )

        def gather_words(a, lo, hi):
            nc.vector.tensor_copy(
                out=slot_words[a][:, lo:hi],
                in_=words[a][:].bitcast(U32).indirect(offs_sb[:, lo // 16 : hi // 16]),
            )

        for a in range(PASSES):
            for (lo, hi), share in zip(HALVES, VECTOR_TOKENS[a]):
                cut = lo + share
                if lo < cut:
                    interleave(nc.vector.tensor_copy, grouped[a], raw[a], lo, cut)
                if cut < hi:
                    interleave(nc.scalar.copy, grouped[a], raw[a], cut, hi)
                if a < PASSES - 1:
                    quantize(a, lo, hi)
            if a < PASSES - 1:
                gather_words(a, 0, SLOTS)
            else:
                quantize(a, 0, T)

        for lo, hi in zip(SCALE_CUTS[:-1], SCALE_CUTS[1:]):
            nc.vector.tensor_copy(out=slot_scales[:, lo:hi], in_=scales[:].indirect(offs_sb[:, lo // 16 : hi // 16]))
            for e in range(lo // C, hi // C):
                for a in range(PASSES - 1):
                    multiply(a, e)
        for lo, hi in zip(LAST_CUTS[:-1], LAST_CUTS[1:]):
            gather_words(PASSES - 1, lo, hi)
            for e in range(lo // C, hi // C):
                multiply(PASSES - 1, e)
                cols = slice(e * C, (e + 1) * C)
                if e < E - 2:
                    nc.scalar.activation(out=y[:, cols], in_=acc[e][:], func=IDENTITY, bias=bias[:, e : e + 1])
                else:
                    nc.vector.tensor_scalar(out=y[:, cols], in0=acc[e][:], scalar1=bias[:, e : e + 1], scalar2=None, op0=ADD)

        nc.vector.tensor_tensor(out=part1[:], in0=y[:].indirect(pos1_sb[:]), in1=gates[:, 0, :], op=MULT)
        for lo, hi in HALVES:
            nc.vector.tensor_tensor(
                out=part2[:, lo:hi],
                in0=y[:].indirect(pos2_sb[:, lo // 16 : hi // 16]),
                in1=gates[:, 1, lo:hi],
                op=MULT,
            )
        for lo, hi in HALVES:
            nc.vector.tensor_tensor(out=total[:, lo:hi], in0=part1[:, lo:hi], in1=part2[:, lo:hi], op=ADD)
            nc.sync.dma_start(out=out[:, lo:hi], in_=total[:, lo:hi])
